import numpy as np
import ml_dtypes


def mxq(x, axis, fmt="e4m3"):
    dtype, down = {"e4m3": (ml_dtypes.float8_e4m3fn, 7), "e5m2": (ml_dtypes.float8_e5m2, 14)}[fmt]
    v = np.moveaxis(np.asarray(x, np.float32).astype(ml_dtypes.bfloat16).astype(np.float64), axis, -1)
    blocks = v.reshape(v.shape[:-1] + (-1, 32))
    amax = np.abs(blocks).max(-1, keepdims=True)
    byte = np.maximum(np.where(amax > 0, np.frexp(amax)[1] - 1 + 127, 0) - down, 1)
    scale = np.exp2(byte - 127.0)
    codes = (blocks / scale).astype(np.float32).astype(dtype).astype(np.float64)
    return np.moveaxis((codes * scale).reshape(v.shape), -1, axis)


WIDE = False


def mx_kscale(k):
    if not WIDE:
        return np.ones(k)
    levels = np.array([10, -10, 5, -5, 0])
    if k % 512:
        return np.exp2(np.random.permutation(np.resize(levels, k // 32))).repeat(32)
    a = np.empty((k // 512, 16))
    for p in range(k // 512):
        a[p, :8] = np.random.permutation(np.resize(levels, 8))
        for g in range(8):
            far = levels[np.abs(levels - a[p, g]) >= 10]
            a[p, g + 8] = far[np.random.randint(len(far))]
    return np.exp2(a.ravel()).repeat(32)


def f64(x):
    return np.asarray(x).astype(np.float64)


def striped(idx):
    return np.tile(idx.reshape(-1, 16).T, (8, 1)).astype(np.uint16)


def unstriped(offs):
    return offs[:16].T.reshape(-1).astype(np.int64)


E2M1 = np.array([0.0, 0.5, 1.0, 1.5, 2.0, 3.0, 4.0, 6.0, -0.0, -0.5, -1.0, -1.5, -2.0, -3.0, -4.0, -6.0])


def pack_weight(w, fmt):
    k, n = w.shape
    w = f64(np.asarray(w, np.float32).astype(ml_dtypes.bfloat16)).reshape(k // 32, 32, n)
    amax = np.abs(w).max(1)
    if fmt == "e4m3":
        byte = np.frexp(amax)[1] - 1 + 127 - 7
    else:
        mant, ex = np.frexp(amax / 6.0)
        byte = np.where(mant > 0.5, ex, ex - 1) + 127
    byte = np.clip(np.where(amax > 0, byte, 1), 1, 254)
    scaled = (w * np.exp2(127.0 - byte)[:, None, :]).reshape(k, n).astype(np.float32)
    by_word = np.ascontiguousarray(scaled.reshape(k // 512, 128, 4, n).transpose(0, 1, 3, 2))
    if fmt == "e4m3":
        words = by_word.astype(ml_dtypes.float8_e4m3fn).view(np.uint8)
    else:
        c = by_word.astype(ml_dtypes.float4_e2m1fn).view(np.uint8) & 0xF
        words = (c[..., 0::2] | (c[..., 1::2] << 4)).reshape(k // 512, 128, 2 * n)
    return np.ascontiguousarray(words), np.ascontiguousarray(byte.astype(np.uint8).reshape(k // 512, 16, n))


def unpack_weight(words, scales, fmt):
    g, _, n = scales.shape
    words = np.ascontiguousarray(words).reshape(g, 128, n, -1)
    if fmt == "e4m3":
        vals = words.view(ml_dtypes.float8_e4m3fn).astype(np.float64)
    else:
        nib = np.empty((g, 128, n, 4), np.uint8)
        nib[..., 0::2] = words & 0xF
        nib[..., 1::2] = words >> 4
        vals = E2M1[nib]
    vals = vals * np.repeat(np.exp2(scales.astype(np.float64) - 127.0), 8, axis=1)[..., None]
    return vals.transpose(0, 1, 3, 2).reshape(g * 512, n)


def pack_table(v):
    words, scales = pack_weight(v, "e4m3")
    return np.concatenate([words.reshape(words.shape[0], -1), scales.reshape(scales.shape[0], -1)], axis=1)


def unpack_table(tab):
    g, t = tab.shape[0], tab.shape[1] // 528
    return unpack_weight(tab[:, :512 * t].reshape(g, 128, t, 4), tab[:, 512 * t:].reshape(g, 16, t), "e4m3")


def split(x):
    m, e = np.frexp(f64(x))
    hi = np.ldexp(np.trunc(16.0 * m) / 16.0, e)
    return hi, f64(x) - hi


def gelu(v):
    return 0.5 * v * (1.0 + np.tanh(np.sqrt(2.0 / np.pi) * (v + 0.044715 * v**3)))


K, M, T, S = 1024, 128, 2048, 512


def setup_inputs():
    n = np.random.standard_normal
    s = mx_kscale(K)[:, None]
    return {
        "tab": pack_table(n((K, T)) * s),
        "w": (n((K, M)) / np.sqrt(K) / s).astype(np.float32),
        "b": (0.3 * n(128)).astype(np.float32),
        "offs": striped(np.random.permutation(T)[:S]),
    }


def reference(tab, w, b, offs):
    tab_ = unpack_table(tab)[:, unstriped(offs)]
    w_hi, w_lo = split(w)
    w_hi_, w_lo_ = mxq(w_hi, 0, "e4m3"), mxq(w_lo, 0, "e4m3")
    y = tab_.T @ w_hi_ + tab_.T @ w_lo_
    return gelu(y + f64(b)[None, :])

@@ -1,0 +1,159 @@
+from contextlib import ExitStack
+
+import concourse.mybir as mybir
+from concourse.masks import make_identity
+
+K, N, T, S = 1024, 128, 2048, 512
+P = 128
+PASSES = 2
+PACK = 4
+GROUPS = S // P
+FLOPS = 2 * 2 * S * N * K
+
+F32 = mybir.dt.float32
+BF16 = mybir.dt.bfloat16
+I32 = mybir.dt.int32
+U32 = mybir.dt.uint32
+U16 = mybir.dt.uint16
+U8 = mybir.dt.uint8
+FP8X4 = mybir.dt.float8_e4m3fn_x4
+
+ALU = mybir.AluOpType
+GELU = mybir.ActivationFunctionType.Gelu_apprx_tanh
+HI_MASK = -983056
+
+
+def tile_list_tabw_tm_hl_gelu_kernel(tc, tab, w, b, offs, out):
+    nc = tc.nc
+    with ExitStack() as ctx:
+        keep = ctx.enter_context(tc.tile_pool(name="keep", bufs=1))
+        psum = ctx.enter_context(tc.psum_pool(name="psum", bufs=1))
+
+        offsets = keep.tile([P, S // 16], U16, name="offsets")
+        nc.sync.dma_start(offsets[:], offs)
+
+        table_scales = keep.tile([P, T // 4], I32, name="table_scales", align_bytes=64)
+        nc.vector.memset(table_scales[:], 0)
+
+        w_raw = [keep.tile([P, PACK, N], F32, name=f"w_raw{a}", align_bytes=64) for a in range(PASSES)]
+        w_view = w.rearrange("(a p j) n -> a p j n", p=P, j=PACK)
+        for a in range(PASSES):
+            nc.sync.dma_start(out=w_raw[a][:], in_=w_view[a])
+
+        for q in range(4):
+            rows = tab[:, 512 * T + 4 * q * T : 512 * T + 4 * (q + 1) * T]
+            nc.scalar.dma_start(
+                out=table_scales[32 * q : 32 * q + 8, :],
+                in_=rows.rearrange("a (r t) -> a r t", r=4).bitcast(I32),
+            )
+
+        bias_col = keep.tile([P, 1], F32, name="bias_col")
+        nc.gpsimd.dma_start(out=bias_col[:], in_=b.rearrange("(n o) -> n o", o=1))
+
+        table = [keep.tile([P, T], I32, name=f"table{a}", align_bytes=64) for a in range(PASSES)]
+        for a in range(PASSES):
+            nc.sync.dma_start(
+                out=table[a][:],
+                in_=tab[a, 0 : 512 * T].rearrange("(p x) -> p x", p=P).bitcast(I32),
+            )
+
+        warm = keep.tile([P, 8], F32, name="warm")
+        warm_out = keep.tile([P, 8], F32, name="warm_out")
+        nc.gpsimd.memset(warm[:], 0.0)
+        nc.scalar.activation(warm_out[:], warm[:], GELU)
+
+        ident = keep.tile([P, P], F32, name="ident")
+        make_identity(nc, ident[:])
+
+        picked_scales = keep.tile([P, S], U8, name="picked_scales", align_bytes=64)
+        nc.vector.tensor_copy(picked_scales[:], table_scales[:].bitcast(U8).indirect(offsets[:]))
+
+        cut = [keep.tile([P, N, PACK], BF16, name=f"cut{a}", align_bytes=64) for a in range(PASSES)]
+        parts = [keep.tile([P, 2, N, PACK], BF16, name=f"parts{a}", align_bytes=64) for a in range(PASSES)]
+        w_codes = [keep.tile([P, 2 * N], U32, name=f"w_codes{a}", align_bytes=64) for a in range(PASSES)]
+        w_scales = [keep.tile([P, 2 * N], U8, name=f"w_scales{a}", align_bytes=64) for a in range(PASSES)]
+        picked = [keep.tile([P, S], U32, name=f"picked{a}", align_bytes=64) for a in range(PASSES)]
+
+        def truncate(a):
+            halves = w_raw[a][:].bitcast(BF16).rearrange("p j (n h) -> p n j h", h=2)
+            nc.scalar.copy(cut[a][:], halves[:, :, :, 1])
+
+        def mask(a):
+            nc.vector.tensor_scalar(
+                out=parts[a][:, 0].rearrange("p n j -> p (n j)").bitcast(I32),
+                in0=cut[a][:].rearrange("p n j -> p (n j)").bitcast(I32),
+                scalar1=HI_MASK,
+                scalar2=None,
+                op0=ALU.bitwise_and,
+            )
+
+        def low(a):
+            nc.vector.tensor_tensor(
+                out=parts[a][:, 1],
+                in0=w_raw[a][:].rearrange("p j n -> p n j"),
+                in1=parts[a][:, 0],
+                op=ALU.subtract,
+            )
+
+        def quantize(a):
+            nc.vector.quantize_mx(
+                out=w_codes[a][:].bitcast(FP8X4),
+                scales=w_scales[a][:],
+                in_=parts[a][:].rearrange("p h n j -> p (h n j)"),
+            )
+
+        def gather(a, half):
+            nc.vector.tensor_copy(
+                picked[a][:, half * 256 : half * 256 + 256],
+                table[a][:].bitcast(U32).indirect(offsets[:, half * 16 : half * 16 + 16]),
+            )
+
+        truncate(0)
+        truncate(1)
+        mask(0)
+        low(0)
+        mask(1)
+        quantize(0)
+        low(1)
+        gather(0, 0)
+        quantize(1)
+        gather(0, 1)
+
+        bias_ps = psum.tile([P, N], F32, name="bias_ps")
+        nc.tensor.transpose(bias_ps[:], bias_col[:, 0:1].to_broadcast([P, P]), ident[:])
+        bias = keep.tile([P, N], F32, name="bias")
+        nc.scalar.copy(bias[:], bias_ps[:])
+
+        sums = [psum.tile([P, N], F32, name=f"sums{g}") for g in range(GROUPS)]
+
+        def multiply(a, g):
+            toks = slice(g * P, g * P + P)
+            for h in range(2):
+                cols = slice(h * N, h * N + N)
+                nc.tensor.matmul_mx(
+                    out=sums[g][:],
+                    lhsT=picked[a][:, toks].bitcast(FP8X4),
+                    lhsT_scale=picked_scales[4 * a : P, toks],
+                    rhs=w_codes[a][:, cols].bitcast(FP8X4),
+                    rhs_scale=w_scales[a][:, cols],
+                    start=(a == 0 and h == 0),
+                    stop=(a == PASSES - 1 and h == 1),
+                )
+
+        for g in range(GROUPS):
+            multiply(0, g)
+
+        pre = keep.tile([P, GROUPS, N], F32, name="pre")
+        res = keep.tile([P, GROUPS, N], F32, name="res")
+        out_view = out.rearrange("(g p) n -> p g n", p=P)
+
+        gather(1, 0)
+        gather(1, 1)
+        for g in range(GROUPS):
+            multiply(1, g)
+            nc.vector.tensor_tensor(out=pre[:, g], in0=sums[g][:], in1=bias[:], op=ALU.add)
+            nc.scalar.activation(res[:, g], pre[:, g], GELU)
+            if g == 1:
+                nc.sync.dma_start(out=out_view[:, 0:2], in_=res[:, 0:2])
+            if g >= 2:
+                (nc.sync if g == 2 else nc.scalar).dma_start(out=out_view[:, g], in_=res[:, g])

@@ -1,7 +1,6 @@
 from contextlib import ExitStack
 
 import concourse.mybir as mybir
-from concourse.masks import make_identity
 
 K, N, T, S = 1024, 128, 2048, 512
 P = 128
@@ -32,23 +31,25 @@ def tile_list_tabw_tm_hl_gelu_kernel(tc, tab, w, b, offs, out):
         offsets = keep.tile([P, S // 16], U16, name="offsets")
         nc.sync.dma_start(offsets[:], offs)
 
-        table_scales = keep.tile([P, T // 4], I32, name="table_scales", align_bytes=64)
+        bias_rows = keep.tile([P, N], F32, name="bias_rows", align_bytes=64)
+        nc.vector.memset(bias_rows[:], 0.0)
+        nc.sync.dma_start(out=bias_rows[0:P:32, :], in_=b.partition_broadcast(4))
+
+        table_scales = keep.tile([P, T // 4], I32, name="table_scales", tag="parts", align_bytes=64)
         nc.vector.memset(table_scales[:], 0)
+        warm = keep.tile([P, 8], F32, name="warm")
+        warm_out = keep.tile([P, 8], F32, name="warm_out")
+        nc.vector.memset(warm[:], 0.0)
+        nc.scalar.activation(warm_out[:], warm[:], GELU)
 
-        w_raw = [keep.tile([P, PACK, N], F32, name=f"w_raw{a}", align_bytes=64) for a in range(PASSES)]
-        w_view = w.rearrange("(a p j) n -> a p j n", p=P, j=PACK)
-        for a in range(PASSES):
-            nc.sync.dma_start(out=w_raw[a][:], in_=w_view[a])
-
+        w_raw = keep.tile([P, PASSES, PACK, N], F32, name="w_raw", align_bytes=64)
+        nc.sync.dma_start(out=w_raw[:], in_=w.rearrange("(a p j) n -> p a j n", p=P, j=PACK))
         for q in range(4):
             rows = tab[:, 512 * T + 4 * q * T : 512 * T + 4 * (q + 1) * T]
-            nc.scalar.dma_start(
+            nc.sync.dma_start(
                 out=table_scales[32 * q : 32 * q + 8, :],
                 in_=rows.rearrange("a (r t) -> a r t", r=4).bitcast(I32),
             )
-
-        bias_col = keep.tile([P, 1], F32, name="bias_col")
-        nc.gpsimd.dma_start(out=bias_col[:], in_=b.rearrange("(n o) -> n o", o=1))
 
         table = [keep.tile([P, T], I32, name=f"table{a}", align_bytes=64) for a in range(PASSES)]
         for a in range(PASSES):
@@ -57,41 +58,41 @@ def tile_list_tabw_tm_hl_gelu_kernel(tc, tab, w, b, offs, out):
                 in_=tab[a, 0 : 512 * T].rearrange("(p x) -> p x", p=P).bitcast(I32),
             )
 
-        warm = keep.tile([P, 8], F32, name="warm")
-        warm_out = keep.tile([P, 8], F32, name="warm_out")
-        nc.gpsimd.memset(warm[:], 0.0)
-        nc.scalar.activation(warm_out[:], warm[:], GELU)
-
-        ident = keep.tile([P, P], F32, name="ident")
-        make_identity(nc, ident[:])
-
+        bias_down = keep.tile([P, N], F32, name="bias_down", align_bytes=64)
+        bias_wide = keep.tile([P, N], F32, name="bias_wide", align_bytes=64)
+        bias = keep.tile([P, N], F32, name="bias", align_bytes=64)
+        nc.vector.transpose(bias_down[:], bias_rows[:])
+        nc.scalar.copy(
+            bias_wide[:].rearrange("p (c i) -> p c i", i=32),
+            bias_down[:].rearrange("p (c i) -> p c i", i=32)[:, :, 0:1].to_broadcast([P, 4, 32]),
+        )
         picked_scales = keep.tile([P, S], U8, name="picked_scales", align_bytes=64)
         nc.vector.tensor_copy(picked_scales[:], table_scales[:].bitcast(U8).indirect(offsets[:]))
 
-        cut = [keep.tile([P, N, PACK], BF16, name=f"cut{a}", align_bytes=64) for a in range(PASSES)]
-        parts = [keep.tile([P, 2, N, PACK], BF16, name=f"parts{a}", align_bytes=64) for a in range(PASSES)]
+        cut = keep.tile([P, PASSES, N, PACK], BF16, name="cut", tag="cut", align_bytes=64)
+        parts = keep.tile([P, PASSES, 2, N, PACK], BF16, name="parts", tag="parts", align_bytes=64)
         w_codes = [keep.tile([P, 2 * N], U32, name=f"w_codes{a}", align_bytes=64) for a in range(PASSES)]
         w_scales = [keep.tile([P, 2 * N], U8, name=f"w_scales{a}", align_bytes=64) for a in range(PASSES)]
-        picked = [keep.tile([P, S], U32, name=f"picked{a}", align_bytes=64) for a in range(PASSES)]
+        picked = []
 
         def truncate(a):
-            halves = w_raw[a][:].bitcast(BF16).rearrange("p j (n h) -> p n j h", h=2)
-            nc.scalar.copy(cut[a][:], halves[:, :, :, 1])
+            halves = w_raw[:, a].bitcast(BF16).rearrange("p j (n h) -> p n j h", h=2)
+            nc.scalar.copy(cut[:, a], halves[:, :, :, 1])
 
         def mask(a):
             nc.vector.tensor_scalar(
-                out=parts[a][:, 0].rearrange("p n j -> p (n j)").bitcast(I32),
-                in0=cut[a][:].rearrange("p n j -> p (n j)").bitcast(I32),
+                out=parts[:, a, 0].rearrange("p n j -> p (n j)").bitcast(I32),
+                in0=cut[:, a].rearrange("p n j -> p (n j)").bitcast(I32),
                 scalar1=HI_MASK,
                 scalar2=None,
                 op0=ALU.bitwise_and,
             )
 
-        def low(a):
-            nc.vector.tensor_tensor(
-                out=parts[a][:, 1],
-                in0=w_raw[a][:].rearrange("p j n -> p n j"),
-                in1=parts[a][:, 0],
+        def low(a, engine):
+            engine.tensor_tensor(
+                out=parts[:, a, 1],
+                in0=w_raw[:, a].rearrange("p j n -> p n j"),
+                in1=parts[:, a, 0],
                 op=ALU.subtract,
             )
 
@@ -99,7 +100,7 @@ def tile_list_tabw_tm_hl_gelu_kernel(tc, tab, w, b, offs, out):
             nc.vector.quantize_mx(
                 out=w_codes[a][:].bitcast(FP8X4),
                 scales=w_scales[a][:],
-                in_=parts[a][:].rearrange("p h n j -> p (h n j)"),
+                in_=parts[:, a].rearrange("p h n j -> p (h n j)"),
             )
 
         def gather(a, half):
@@ -111,18 +112,17 @@ def tile_list_tabw_tm_hl_gelu_kernel(tc, tab, w, b, offs, out):
         truncate(0)
         truncate(1)
         mask(0)
-        low(0)
         mask(1)
+        low(0, nc.vector)
+        low(1, nc.vector)
         quantize(0)
-        low(1)
+        nc.vector.transpose(bias[:], bias_wide[:])
+        picked.append(keep.tile([P, S], U32, name="picked0", tag="cut", align_bytes=64))
         gather(0, 0)
         quantize(1)
         gather(0, 1)
+        picked.append(keep.tile([P, S], U32, name="picked1", tag="parts", align_bytes=64))
 
-        bias_ps = psum.tile([P, N], F32, name="bias_ps")
-        nc.tensor.transpose(bias_ps[:], bias_col[:, 0:1].to_broadcast([P, P]), ident[:])
-        bias = keep.tile([P, N], F32, name="bias")
-        nc.scalar.copy(bias[:], bias_ps[:])
 
         sums = [psum.tile([P, N], F32, name=f"sums{g}") for g in range(GROUPS)]
 

from contextlib import ExitStack

import concourse.mybir as mybir

K, N, T, S = 1024, 128, 2048, 512
P = 128
PASSES = 2
PACK = 4
GROUPS = S // P
FLOPS = 2 * 2 * S * N * K

F32 = mybir.dt.float32
BF16 = mybir.dt.bfloat16
I32 = mybir.dt.int32
U32 = mybir.dt.uint32
U16 = mybir.dt.uint16
U8 = mybir.dt.uint8
FP8X4 = mybir.dt.float8_e4m3fn_x4

ALU = mybir.AluOpType
GELU = mybir.ActivationFunctionType.Gelu_apprx_tanh
HI_MASK = -983056


def tile_list_tabw_tm_hl_gelu_kernel(tc, tab, w, b, offs, out):
    nc = tc.nc
    with ExitStack() as ctx:
        keep = ctx.enter_context(tc.tile_pool(name="keep", bufs=1))
        psum = ctx.enter_context(tc.psum_pool(name="psum", bufs=1))

        offsets = keep.tile([P, S // 16], U16, name="offsets")
        nc.sync.dma_start(offsets[:], offs)

        bias_rows = keep.tile([P, N], F32, name="bias_rows", align_bytes=64)
        nc.vector.memset(bias_rows[:], 0.0)
        nc.sync.dma_start(out=bias_rows[0:P:32, :], in_=b.partition_broadcast(4))

        table_scales = keep.tile([P, T // 4], I32, name="table_scales", tag="parts", align_bytes=64)
        nc.vector.memset(table_scales[:], 0)
        warm = keep.tile([P, 8], F32, name="warm")
        warm_out = keep.tile([P, 8], F32, name="warm_out")
        nc.vector.memset(warm[:], 0.0)
        nc.scalar.activation(warm_out[:], warm[:], GELU)

        w_raw = keep.tile([P, PASSES, PACK, N], F32, name="w_raw", align_bytes=64)
        nc.sync.dma_start(out=w_raw[:], in_=w.rearrange("(a p j) n -> p a j n", p=P, j=PACK))
        for q in range(4):
            rows = tab[:, 512 * T + 4 * q * T : 512 * T + 4 * (q + 1) * T]
            nc.sync.dma_start(
                out=table_scales[32 * q : 32 * q + 8, :],
                in_=rows.rearrange("a (r t) -> a r t", r=4).bitcast(I32),
            )

        table = [keep.tile([P, T], I32, name=f"table{a}", align_bytes=64) for a in range(PASSES)]
        for a in range(PASSES):
            nc.sync.dma_start(
                out=table[a][:],
                in_=tab[a, 0 : 512 * T].rearrange("(p x) -> p x", p=P).bitcast(I32),
            )

        bias_down = keep.tile([P, N], F32, name="bias_down", align_bytes=64)
        bias_wide = keep.tile([P, N], F32, name="bias_wide", align_bytes=64)
        bias = keep.tile([P, N], F32, name="bias", align_bytes=64)
        nc.vector.transpose(bias_down[:], bias_rows[:])
        nc.scalar.copy(
            bias_wide[:].rearrange("p (c i) -> p c i", i=32),
            bias_down[:].rearrange("p (c i) -> p c i", i=32)[:, :, 0:1].to_broadcast([P, 4, 32]),
        )
        picked_scales = keep.tile([P, S], U8, name="picked_scales", align_bytes=64)
        nc.vector.tensor_copy(picked_scales[:], table_scales[:].bitcast(U8).indirect(offsets[:]))

        cut = keep.tile([P, PASSES, N, PACK], BF16, name="cut", tag="cut", align_bytes=64)
        parts = keep.tile([P, PASSES, 2, N, PACK], BF16, name="parts", tag="parts", align_bytes=64)
        w_codes = [keep.tile([P, 2 * N], U32, name=f"w_codes{a}", align_bytes=64) for a in range(PASSES)]
        w_scales = [keep.tile([P, 2 * N], U8, name=f"w_scales{a}", align_bytes=64) for a in range(PASSES)]
        picked = []

        def truncate(a):
            halves = w_raw[:, a].bitcast(BF16).rearrange("p j (n h) -> p n j h", h=2)
            nc.scalar.copy(cut[:, a], halves[:, :, :, 1])

        def mask(a):
            nc.vector.tensor_scalar(
                out=parts[:, a, 0].rearrange("p n j -> p (n j)").bitcast(I32),
                in0=cut[:, a].rearrange("p n j -> p (n j)").bitcast(I32),
                scalar1=HI_MASK,
                scalar2=None,
                op0=ALU.bitwise_and,
            )

        def low(a, engine):
            engine.tensor_tensor(
                out=parts[:, a, 1],
                in0=w_raw[:, a].rearrange("p j n -> p n j"),
                in1=parts[:, a, 0],
                op=ALU.subtract,
            )

        def quantize(a):
            nc.vector.quantize_mx(
                out=w_codes[a][:].bitcast(FP8X4),
                scales=w_scales[a][:],
                in_=parts[:, a].rearrange("p h n j -> p (h n j)"),
            )

        def gather(a, half):
            nc.vector.tensor_copy(
                picked[a][:, half * 256 : half * 256 + 256],
                table[a][:].bitcast(U32).indirect(offsets[:, half * 16 : half * 16 + 16]),
            )

        truncate(0)
        truncate(1)
        mask(0)
        mask(1)
        low(0, nc.vector)
        low(1, nc.vector)
        quantize(0)
        nc.vector.transpose(bias[:], bias_wide[:])
        picked.append(keep.tile([P, S], U32, name="picked0", tag="cut", align_bytes=64))
        gather(0, 0)
        quantize(1)
        gather(0, 1)
        picked.append(keep.tile([P, S], U32, name="picked1", tag="parts", align_bytes=64))


        sums = [psum.tile([P, N], F32, name=f"sums{g}") for g in range(GROUPS)]

        def multiply(a, g):
            toks = slice(g * P, g * P + P)
            for h in range(2):
                cols = slice(h * N, h * N + N)
                nc.tensor.matmul_mx(
                    out=sums[g][:],
                    lhsT=picked[a][:, toks].bitcast(FP8X4),
                    lhsT_scale=picked_scales[4 * a : P, toks],
                    rhs=w_codes[a][:, cols].bitcast(FP8X4),
                    rhs_scale=w_scales[a][:, cols],
                    start=(a == 0 and h == 0),
                    stop=(a == PASSES - 1 and h == 1),
                )

        for g in range(GROUPS):
            multiply(0, g)

        pre = keep.tile([P, GROUPS, N], F32, name="pre")
        res = keep.tile([P, GROUPS, N], F32, name="res")
        out_view = out.rearrange("(g p) n -> p g n", p=P)

        gather(1, 0)
        gather(1, 1)
        for g in range(GROUPS):
            multiply(1, g)
            nc.vector.tensor_tensor(out=pre[:, g], in0=sums[g][:], in1=bias[:], op=ALU.add)
            nc.scalar.activation(res[:, g], pre[:, g], GELU)
            if g == 1:
                nc.sync.dma_start(out=out_view[:, 0:2], in_=res[:, 0:2])
            if g >= 2:
                (nc.sync if g == 2 else nc.scalar).dma_start(out=out_view[:, g], in_=res[:, g])
